import numpy as np
import ml_dtypes


def mxq(x, axis, fmt="e4m3"):
    dtype, down = {"e4m3": (ml_dtypes.float8_e4m3fn, 7), "e5m2": (ml_dtypes.float8_e5m2, 14)}[fmt]
    v = np.moveaxis(np.asarray(x, np.float32).astype(ml_dtypes.bfloat16).astype(np.float64), axis, -1)
    blocks = v.reshape(v.shape[:-1] + (-1, 32))
    amax = np.abs(blocks).max(-1, keepdims=True)
    byte = np.maximum(np.where(amax > 0, np.frexp(amax)[1] - 1 + 127, 0) - down, 1)
    scale = np.exp2(byte - 127.0)
    codes = (blocks / scale).astype(np.float32).astype(dtype).astype(np.float64)
    return np.moveaxis((codes * scale).reshape(v.shape), -1, axis)


WIDE = False


def mx_kscale(k):
    if not WIDE:
        return np.ones(k)
    levels = np.array([10, -10, 5, -5, 0])
    if k % 512:
        return np.exp2(np.random.permutation(np.resize(levels, k // 32))).repeat(32)
    a = np.empty((k // 512, 16))
    for p in range(k // 512):
        a[p, :8] = np.random.permutation(np.resize(levels, 8))
        for g in range(8):
            far = levels[np.abs(levels - a[p, g]) >= 10]
            a[p, g + 8] = far[np.random.randint(len(far))]
    return np.exp2(a.ravel()).repeat(32)


def f64(x):
    return np.asarray(x).astype(np.float64)


def striped(idx):
    return np.tile(np.asarray(idx).reshape(-1, 16).T, (8, 1)).astype(np.uint16)


def unstriped(offs):
    return offs[:16].T.reshape(-1).astype(np.int64)


E2M1 = np.array([0.0, 0.5, 1.0, 1.5, 2.0, 3.0, 4.0, 6.0, -0.0, -0.5, -1.0, -1.5, -2.0, -3.0, -4.0, -6.0])


def pack_weight(w, fmt):
    k, n = w.shape
    w = f64(np.asarray(w, np.float32).astype(ml_dtypes.bfloat16)).reshape(k // 32, 32, n)
    amax = np.abs(w).max(1)
    if fmt == "e4m3":
        byte = np.frexp(amax)[1] - 1 + 127 - 7
    else:
        mant, ex = np.frexp(amax / 6.0)
        byte = np.where(mant > 0.5, ex, ex - 1) + 127
    byte = np.clip(np.where(amax > 0, byte, 1), 1, 254)
    scaled = (w * np.exp2(127.0 - byte)[:, None, :]).reshape(k, n).astype(np.float32)
    by_word = np.ascontiguousarray(scaled.reshape(k // 512, 128, 4, n).transpose(0, 1, 3, 2))
    if fmt == "e4m3":
        words = by_word.astype(ml_dtypes.float8_e4m3fn).view(np.uint8)
    else:
        c = by_word.astype(ml_dtypes.float4_e2m1fn).view(np.uint8) & 0xF
        words = (c[..., 0::2] | (c[..., 1::2] << 4)).reshape(k // 512, 128, 2 * n)
    return np.ascontiguousarray(words), np.ascontiguousarray(byte.astype(np.uint8).reshape(k // 512, 16, n))


def unpack_weight(words, scales, fmt):
    g, _, n = scales.shape
    words = np.ascontiguousarray(words).reshape(g, 128, n, -1)
    if fmt == "e4m3":
        vals = words.view(ml_dtypes.float8_e4m3fn).astype(np.float64)
    else:
        nib = np.empty((g, 128, n, 4), np.uint8)
        nib[..., 0::2] = words & 0xF
        nib[..., 1::2] = words >> 4
        vals = E2M1[nib]
    vals = vals * np.repeat(np.exp2(scales.astype(np.float64) - 127.0), 8, axis=1)[..., None]
    return vals.transpose(0, 1, 3, 2).reshape(g * 512, n)


K, L, T, J, N = 1024, 512, 1024, 512, 512


def setup_inputs():
    n = np.random.standard_normal
    idx = np.random.permutation(T)[:J]
    fk = mx_kscale(K)
    fl = mx_kscale(L)
    xtp = pack_weight(n((K, T)) / fk[:, None], "e4m3")
    wsp = pack_weight(n((K, N)) * 1 / np.sqrt(K) * fk[:, None], "e2m1")
    xep = pack_weight(n((L, J)) / fl[:, None], "e4m3")
    return {
        "xt_words": xtp[0],
        "xt_scales": xtp[1],
        "ws_words": wsp[0],
        "ws_scales": wsp[1],
        "xe_words": xep[0],
        "xe_scales": xep[1],
        "we": (n((L, N)) * 1 / np.sqrt(L) * fl[:, None]).astype(np.float32),
        "bd": (np.random.uniform(0.3, 1.0, (N, 1))).astype(np.float32),
        "rw": (np.random.uniform(0.5, 2.0, (1, J))).astype(np.float32),
        "offs": striped(idx),
    }


def reference(xt_words, xt_scales, ws_words, ws_scales, xe_words, xe_scales, we, bd, rw, offs):
    idx = unstriped(offs)
    xtu = unpack_weight(xt_words, xt_scales, "e4m3")
    wsu = unpack_weight(ws_words, ws_scales, "e2m1")
    xeu = unpack_weight(xe_words, xe_scales, "e4m3")
    u = wsu.T @ xtu
    weq = mxq(f64(we), 0, "e4m3")
    p = weq.T @ xeu
    h1 = np.minimum(p, u[:, idx] + f64(bd))
    y = np.maximum(h1, u[:, idx] - f64(bd)) * f64(rw)
    return y

@@ -1,0 +1,184 @@
+from contextlib import ExitStack
+
+import concourse.mybir as mybir
+from concourse.masks import make_identity
+
+K, L, T, J, N = 1024, 512, 1024, 512, 512
+FLOPS = 2 * N * (K * T + L * J)
+
+F32 = mybir.dt.float32
+BF16 = mybir.dt.bfloat16
+I32 = mybir.dt.int32
+U32 = mybir.dt.uint32
+U16 = mybir.dt.uint16
+U8 = mybir.dt.uint8
+FP8X4 = mybir.dt.float8_e4m3fn_x4
+FP4X4 = mybir.dt.float4_e2m1fn_x4
+ALU = mybir.AluOpType
+
+P = 128
+PACK = 4
+BANK = 512
+PASSES = K // (P * PACK)
+BLOCKS = N // P
+HALVES = T // BANK
+WE_PARTS = 2
+WE_COLS = N // WE_PARTS
+
+
+def tile_moe_expert_held_near_shared_kernel(
+    tc, xt_words, xt_scales, ws_words, ws_scales, xe_words, xe_scales, we, bd, rw, offs, out
+):
+    nc = tc.nc
+    with ExitStack() as ctx:
+        keep = ctx.enter_context(tc.tile_pool(name="keep", bufs=1))
+        psum = ctx.enter_context(tc.psum_pool(name="psum", bufs=1))
+
+        offsets = keep.tile([P, J // 16], U16, name="offsets")
+        xt_plane = keep.tile([P, PASSES, T], U8, name="xt_plane", align_bytes=64)
+        ws_plane = keep.tile([P, PASSES, N], U8, name="ws_plane", align_bytes=64)
+        xe_plane = keep.tile([P, 1, J], U8, name="xe_plane", align_bytes=64)
+        ws_codes = keep.tile([P, PASSES, 2 * N], U8, name="ws_codes", align_bytes=64)
+        xt_codes = [keep.tile([P, PASSES, BANK], U32, name="xt_codes%d" % h, align_bytes=64) for h in range(HALVES)]
+        xe_codes = keep.tile([P, J], U32, name="xe_codes", align_bytes=64)
+        we_raw = [keep.tile([P, PACK, WE_COLS], F32, name="we_raw%d" % a) for a in range(WE_PARTS)]
+        we_bf16 = [keep.tile([P, WE_COLS, PACK], BF16, name="we_bf16%d" % a, align_bytes=64) for a in range(WE_PARTS)]
+        we_codes = [keep.tile([P, WE_COLS], U32, name="we_codes%d" % a, align_bytes=64) for a in range(WE_PARTS)]
+        we_plane = [keep.tile([P, WE_COLS], U8, name="we_plane%d" % a, align_bytes=64) for a in range(WE_PARTS)]
+        vec_rows = keep.tile([P, P], F32, name="vec_rows")
+        vec_cols = keep.tile([P, 2 * BLOCKS], F32, name="vec_cols")
+        ident = keep.tile([P, P], F32, name="ident")
+        u_sb = [keep.tile([P, T], F32, name="u%d" % b) for b in range(BLOCKS)]
+        listed = [keep.tile([P, J], F32, name="listed%d" % b) for b in range(BLOCKS)]
+        capped = [keep.tile([P, J], F32, name="capped%d" % b) for b in range(BLOCKS)]
+        held = [keep.tile([P, J], F32, name="held%d" % b) for b in range(BLOCKS)]
+        result = [keep.tile([P, J], F32, name="result%d" % b) for b in range(BLOCKS)]
+
+        def load_scale_rows(engine, plane, scales, r):
+            src = scales.rearrange("z (q r) c -> r q z c", r=PACK)[r]
+            engine.dma_start(out=plane[r:P:32, :, :].bitcast(I32), in_=src.bitcast(I32))
+
+        nc.vector.memset(xt_plane[:].bitcast(I32), 0)
+        nc.vector.memset(ws_plane[:].bitcast(I32), 0)
+        for r in range(PACK):
+            load_scale_rows(nc.scalar, xt_plane, xt_scales, r)
+        for r in range(PACK - 1):
+            load_scale_rows(nc.scalar, ws_plane, ws_scales, r)
+
+        nc.sync.dma_start(out=ws_codes[:].bitcast(I32), in_=ws_words.rearrange("z p c -> p z c").bitcast(I32))
+        xt_rows = xt_words.rearrange("z p c r -> p z (c r)")
+        for h in range(HALVES):
+            cols = slice(h * BANK * PACK, (h + 1) * BANK * PACK)
+            nc.sync.dma_start(out=xt_codes[h][:].bitcast(I32), in_=xt_rows[:, :, cols].bitcast(I32))
+        load_scale_rows(nc.sync, ws_plane, ws_scales, PACK - 1)
+        nc.sync.dma_start(offsets[:], offs)
+
+        we_rows = we.rearrange("(p j) n -> p j n", j=PACK)
+        nc.vector.memset(xe_plane[:].bitcast(I32), 0)
+        nc.vector.memset(vec_rows[:], 0.0)
+        nc.sync.dma_start(out=we_raw[0][:], in_=we_rows[:, :, 0:WE_COLS])
+        nc.sync.dma_start(out=xe_codes[:].bitcast(I32), in_=xe_words[0].rearrange("p c r -> p (c r)").bitcast(I32))
+        for r in range(PACK):
+            load_scale_rows(nc.sync, xe_plane, xe_scales, r)
+        nc.sync.dma_start(out=vec_rows[0:BLOCKS, :], in_=bd.rearrange("(c p) o -> c (p o)", p=P))
+        nc.sync.dma_start(out=vec_rows[BLOCKS : 2 * BLOCKS, :], in_=rw.rearrange("o (c p) -> (o c) p", p=P))
+        nc.sync.dma_start(out=we_raw[1][:], in_=we_rows[:, :, WE_COLS:N])
+        make_identity(nc, ident[:])
+
+        def shared_product(b):
+            for h in range(HALVES):
+                acc = psum.tile([P, BANK], F32, name="u_acc", tag="u_acc", bufs=5)
+                for z in range(PASSES):
+                    nc.tensor.matmul_mx(
+                        out=acc[:],
+                        lhsT=ws_codes[:, z, 2 * P * b : 2 * P * (b + 1)].bitcast(FP4X4),
+                        lhsT_scale=ws_plane[:, z, P * b : P * (b + 1)],
+                        rhs=xt_codes[h][:, z, :].bitcast(FP8X4),
+                        rhs_scale=xt_plane[:, z, BANK * h : BANK * (h + 1)],
+                        start=(z == 0),
+                        stop=(z == PASSES - 1),
+                    )
+                nc.scalar.copy(out=u_sb[b][:, BANK * h : BANK * (h + 1)], in_=acc[:])
+
+        def gather(b):
+            nc.vector.tensor_copy(out=listed[b][:], in_=u_sb[b][:].indirect(offsets[:]))
+
+        def round_we(a):
+            nc.scalar.copy(
+                out=we_bf16[a][:].rearrange("p (c i) j -> p c j i", i=4),
+                in_=we_raw[a][:].rearrange("p j (c i) -> p c j i", i=4),
+            )
+
+        def quantize_we(a):
+            nc.vector.quantize_mx(
+                out=we_codes[a][:].bitcast(FP8X4),
+                scales=we_plane[a][:],
+                in_=we_bf16[a][:].rearrange("p c j -> p (c j)"),
+            )
+
+        def expert_product(b):
+            a, c = divmod(b * P, WE_COLS)
+            acc = psum.tile([P, J], F32, name="p_acc", tag="p_acc", bufs=2)
+            nc.tensor.matmul_mx(
+                out=acc[:],
+                lhsT=we_codes[a][:, c : c + P].bitcast(FP8X4),
+                lhsT_scale=we_plane[a][:, c : c + P],
+                rhs=xe_codes[:].bitcast(FP8X4),
+                rhs_scale=xe_plane[:, 0, :],
+                start=True,
+                stop=True,
+            )
+            return acc
+
+        def cap(b, p_acc):
+            nc.vector.scalar_tensor_tensor(
+                out=capped[b][:], in0=listed[b][:], scalar=vec_cols[:, b : b + 1], in1=p_acc[:], op0=ALU.add, op1=ALU.min
+            )
+
+        def floor(b):
+            nc.vector.scalar_tensor_tensor(
+                out=held[b][:], in0=listed[b][:], scalar=vec_cols[:, b : b + 1], in1=capped[b][:], op0=ALU.subtract, op1=ALU.max
+            )
+
+        def weigh(b, cols, engine):
+            nc.vector.tensor_tensor(out=result[b][:, cols], in0=held[b][:, cols], in1=rw_all[:, cols], op=ALU.mult)
+            engine.dma_start(out=out[P * b : P * (b + 1), cols], in_=result[b][:, cols])
+
+        shared_product(0)
+        gather(0)
+        shared_product(1)
+        gather(1)
+
+        vec_t = psum.tile([P, P], F32, name="vec_t", tag="p_acc", bufs=2)
+        nc.tensor.transpose(vec_t[:], vec_rows[:], ident[:])
+        nc.scalar.copy(out=vec_cols[:], in_=vec_t[:, 0 : 2 * BLOCKS])
+        round_we(0)
+        quantize_we(0)
+        shared_product(2)
+        gather(2)
+        rw_all = psum.tile([P, J], F32, name="rw_all", tag="rw_all", bufs=1)
+        for c in range(J // P):
+            col = vec_cols[:, BLOCKS + c : BLOCKS + c + 1]
+            nc.tensor.transpose(rw_all[:, P * c : P * (c + 1)], col.to_broadcast([P, P]), ident[:])
+        p0 = expert_product(0)
+        p1 = expert_product(1)
+        shared_product(3)
+        round_we(1)
+        cap(0, p0)
+        cap(1, p1)
+        floor(0)
+        floor(1)
+        quantize_we(1)
+        gather(3)
+        p2 = expert_product(2)
+        p3 = expert_product(3)
+        everything = slice(0, J)
+        weigh(0, everything, nc.sync)
+        weigh(1, everything, nc.sync)
+        cap(2, p2)
+        cap(3, p3)
+        floor(2)
+        floor(3)
+        weigh(2, everything, nc.sync)
+        weigh(3, slice(0, J // 2), nc.scalar)
+        weigh(3, slice(J // 2, J), nc.sync)

@@ -42,9 +42,9 @@ def tile_moe_expert_held_near_shared_kernel(
         xt_codes = [keep.tile([P, PASSES, BANK], U32, name="xt_codes%d" % h, align_bytes=64) for h in range(HALVES)]
         xe_codes = keep.tile([P, J], U32, name="xe_codes", align_bytes=64)
         we_raw = [keep.tile([P, PACK, WE_COLS], F32, name="we_raw%d" % a) for a in range(WE_PARTS)]
-        we_bf16 = [keep.tile([P, WE_COLS, PACK], BF16, name="we_bf16%d" % a, align_bytes=64) for a in range(WE_PARTS)]
-        we_codes = [keep.tile([P, WE_COLS], U32, name="we_codes%d" % a, align_bytes=64) for a in range(WE_PARTS)]
-        we_plane = [keep.tile([P, WE_COLS], U8, name="we_plane%d" % a, align_bytes=64) for a in range(WE_PARTS)]
+        we_bf16 = [keep.tile([P, P, PACK], BF16, name="we_bf16%d" % b, align_bytes=64) for b in range(BLOCKS)]
+        we_codes = [keep.tile([P, P], U32, name="we_codes%d" % b, align_bytes=64) for b in range(BLOCKS)]
+        we_plane = [keep.tile([P, P], U8, name="we_plane%d" % b, align_bytes=64) for b in range(BLOCKS)]
         vec_rows = keep.tile([P, P], F32, name="vec_rows")
         vec_cols = keep.tile([P, 2 * BLOCKS], F32, name="vec_cols")
         ident = keep.tile([P, P], F32, name="ident")
@@ -58,25 +58,25 @@ def tile_moe_expert_held_near_shared_kernel(
             src = scales.rearrange("z (q r) c -> r q z c", r=PACK)[r]
             engine.dma_start(out=plane[r:P:32, :, :].bitcast(I32), in_=src.bitcast(I32))
 
-        nc.vector.memset(xt_plane[:].bitcast(I32), 0)
         nc.vector.memset(ws_plane[:].bitcast(I32), 0)
-        for r in range(PACK):
-            load_scale_rows(nc.scalar, xt_plane, xt_scales, r)
-        for r in range(PACK - 1):
-            load_scale_rows(nc.scalar, ws_plane, ws_scales, r)
-
+        nc.vector.memset(xt_plane[:].bitcast(I32), 0)
         nc.sync.dma_start(out=ws_codes[:].bitcast(I32), in_=ws_words.rearrange("z p c -> p z c").bitcast(I32))
+        load_scale_rows(nc.sync, ws_plane, ws_scales, 0)
+        for r in range(1, PACK):
+            load_scale_rows(nc.scalar, ws_plane, ws_scales, r)
+        for r in range(PACK - 1):
+            load_scale_rows(nc.scalar, xt_plane, xt_scales, r)
         xt_rows = xt_words.rearrange("z p c r -> p z (c r)")
         for h in range(HALVES):
             cols = slice(h * BANK * PACK, (h + 1) * BANK * PACK)
             nc.sync.dma_start(out=xt_codes[h][:].bitcast(I32), in_=xt_rows[:, :, cols].bitcast(I32))
-        load_scale_rows(nc.sync, ws_plane, ws_scales, PACK - 1)
-        nc.sync.dma_start(offsets[:], offs)
+        load_scale_rows(nc.sync, xt_plane, xt_scales, PACK - 1)
 
         we_rows = we.rearrange("(p j) n -> p j n", j=PACK)
         nc.vector.memset(xe_plane[:].bitcast(I32), 0)
         nc.vector.memset(vec_rows[:], 0.0)
         nc.sync.dma_start(out=we_raw[0][:], in_=we_rows[:, :, 0:WE_COLS])
+        nc.sync.dma_start(offsets[:], offs)
         nc.sync.dma_start(out=xe_codes[:].bitcast(I32), in_=xe_words[0].rearrange("p c r -> p (c r)").bitcast(I32))
         for r in range(PACK):
             load_scale_rows(nc.sync, xe_plane, xe_scales, r)
@@ -85,44 +85,44 @@ def tile_moe_expert_held_near_shared_kernel(
         nc.sync.dma_start(out=we_raw[1][:], in_=we_rows[:, :, WE_COLS:N])
         make_identity(nc, ident[:])
 
-        def shared_product(b):
-            for h in range(HALVES):
-                acc = psum.tile([P, BANK], F32, name="u_acc", tag="u_acc", bufs=5)
-                for z in range(PASSES):
-                    nc.tensor.matmul_mx(
-                        out=acc[:],
-                        lhsT=ws_codes[:, z, 2 * P * b : 2 * P * (b + 1)].bitcast(FP4X4),
-                        lhsT_scale=ws_plane[:, z, P * b : P * (b + 1)],
-                        rhs=xt_codes[h][:, z, :].bitcast(FP8X4),
-                        rhs_scale=xt_plane[:, z, BANK * h : BANK * (h + 1)],
-                        start=(z == 0),
-                        stop=(z == PASSES - 1),
-                    )
-                nc.scalar.copy(out=u_sb[b][:, BANK * h : BANK * (h + 1)], in_=acc[:])
+        def bank(name):
+            return psum.tile([P, BANK], F32, name=name, tag=name, bufs=1)
+
+        def shared_product(b, h, acc):
+            for z in range(PASSES):
+                nc.tensor.matmul_mx(
+                    out=acc[:],
+                    lhsT=ws_codes[:, z, 2 * P * b : 2 * P * (b + 1)].bitcast(FP4X4),
+                    lhsT_scale=ws_plane[:, z, P * b : P * (b + 1)],
+                    rhs=xt_codes[h][:, z, :].bitcast(FP8X4),
+                    rhs_scale=xt_plane[:, z, BANK * h : BANK * (h + 1)],
+                    start=(z == 0),
+                    stop=(z == PASSES - 1),
+                )
+            nc.scalar.copy(out=u_sb[b][:, BANK * h : BANK * (h + 1)], in_=acc[:])
 
         def gather(b):
             nc.vector.tensor_copy(out=listed[b][:], in_=u_sb[b][:].indirect(offsets[:]))
 
-        def round_we(a):
-            nc.scalar.copy(
-                out=we_bf16[a][:].rearrange("p (c i) j -> p c j i", i=4),
-                in_=we_raw[a][:].rearrange("p j (c i) -> p c j i", i=4),
-            )
-
-        def quantize_we(a):
-            nc.vector.quantize_mx(
-                out=we_codes[a][:].bitcast(FP8X4),
-                scales=we_plane[a][:],
-                in_=we_bf16[a][:].rearrange("p c j -> p (c j)"),
-            )
-
-        def expert_product(b):
+        def round_we(b):
             a, c = divmod(b * P, WE_COLS)
-            acc = psum.tile([P, J], F32, name="p_acc", tag="p_acc", bufs=2)
+            nc.scalar.copy(
+                out=we_bf16[b][:].rearrange("p (c i) j -> p c j i", i=4),
+                in_=we_raw[a][:, :, c : c + P].rearrange("p j (c i) -> p c j i", i=4),
+            )
+
+        def quantize_we(b):
+            nc.vector.quantize_mx(
+                out=we_codes[b][:].bitcast(FP8X4),
+                scales=we_plane[b][:],
+                in_=we_bf16[b][:].rearrange("p c j -> p (c j)"),
+            )
+
+        def expert_product(b, acc):
             nc.tensor.matmul_mx(
                 out=acc[:],
-                lhsT=we_codes[a][:, c : c + P].bitcast(FP8X4),
-                lhsT_scale=we_plane[a][:, c : c + P],
+                lhsT=we_codes[b][:].bitcast(FP8X4),
+                lhsT_scale=we_plane[b][:],
                 rhs=xe_codes[:].bitcast(FP8X4),
                 rhs_scale=xe_plane[:, 0, :],
                 start=True,
@@ -140,45 +140,53 @@ def tile_moe_expert_held_near_shared_kernel(
                 out=held[b][:], in0=listed[b][:], scalar=vec_cols[:, b : b + 1], in1=capped[b][:], op0=ALU.subtract, op1=ALU.max
             )
 
-        def weigh(b, cols, engine):
-            nc.vector.tensor_tensor(out=result[b][:, cols], in0=held[b][:, cols], in1=rw_all[:, cols], op=ALU.mult)
-            engine.dma_start(out=out[P * b : P * (b + 1), cols], in_=result[b][:, cols])
+        def weigh(b, cols, engine, weights, queue):
+            engine.tensor_tensor(out=result[b][:, cols], in0=held[b][:, cols], in1=weights[:, cols], op=ALU.mult)
+            queue.dma_start(out=out[P * b : P * (b + 1), cols], in_=result[b][:, cols])
 
-        shared_product(0)
-        gather(0)
-        shared_product(1)
-        gather(1)
-
-        vec_t = psum.tile([P, P], F32, name="vec_t", tag="p_acc", bufs=2)
-        nc.tensor.transpose(vec_t[:], vec_rows[:], ident[:])
-        nc.scalar.copy(out=vec_cols[:], in_=vec_t[:, 0 : 2 * BLOCKS])
+        everything = slice(0, J)
+        shared_product(0, 0, bank("bank0"))
         round_we(0)
         quantize_we(0)
-        shared_product(2)
-        gather(2)
-        rw_all = psum.tile([P, J], F32, name="rw_all", tag="rw_all", bufs=1)
+        shared_product(0, 1, bank("bank1"))
+        gather(0)
+        shared_product(1, 0, bank("bank2"))
+        shared_product(1, 1, bank("bank3"))
+        gather(1)
+        p0 = expert_product(0, bank("bank3"))
+
+        vec_t = bank("bank6")
+        nc.tensor.transpose(vec_t[:, 0:P], vec_rows[:], ident[:])
+        nc.scalar.copy(out=vec_cols[:], in_=vec_t[:, 0 : 2 * BLOCKS])
+        round_we(1)
+        shared_product(2, 0, bank("bank4"))
+        shared_product(2, 1, bank("bank5"))
+        rw_all = bank("bank7")
         for c in range(J // P):
             col = vec_cols[:, BLOCKS + c : BLOCKS + c + 1]
             nc.tensor.transpose(rw_all[:, P * c : P * (c + 1)], col.to_broadcast([P, P]), ident[:])
-        p0 = expert_product(0)
-        p1 = expert_product(1)
-        shared_product(3)
-        round_we(1)
         cap(0, p0)
-        cap(1, p1)
-        floor(0)
-        floor(1)
         quantize_we(1)
+        floor(0)
+        gather(2)
+        p1 = expert_product(1, bank("bank5"))
+        round_we(2)
+        round_we(3)
+        shared_product(3, 0, bank("bank0"))
+        shared_product(3, 1, bank("bank1"))
+        cap(1, p1)
+        quantize_we(2)
+        weigh(0, everything, nc.vector, rw_all, nc.sync)
+        floor(1)
+        quantize_we(3)
         gather(3)
-        p2 = expert_product(2)
-        p3 = expert_product(3)
-        everything = slice(0, J)
-        weigh(0, everything, nc.sync)
-        weigh(1, everything, nc.sync)
+        weigh(1, everything, nc.vector, rw_all, nc.sync)
+        p2 = expert_product(2, bank("bank1"))
+        p3 = expert_product(3, bank("bank0"))
         cap(2, p2)
         cap(3, p3)
         floor(2)
         floor(3)
-        weigh(2, everything, nc.sync)
-        weigh(3, slice(0, J // 2), nc.scalar)
-        weigh(3, slice(J // 2, J), nc.sync)
+        weigh(2, everything, nc.vector, rw_all, nc.sync)
+        weigh(3, slice(0, J // 2), nc.vector, rw_all, nc.scalar)
+        weigh(3, slice(J // 2, J), nc.vector, rw_all, nc.sync)

from contextlib import ExitStack

import concourse.mybir as mybir
from concourse.masks import make_identity

K, L, T, J, N = 1024, 512, 1024, 512, 512
FLOPS = 2 * N * (K * T + L * J)

F32 = mybir.dt.float32
BF16 = mybir.dt.bfloat16
I32 = mybir.dt.int32
U32 = mybir.dt.uint32
U16 = mybir.dt.uint16
U8 = mybir.dt.uint8
FP8X4 = mybir.dt.float8_e4m3fn_x4
FP4X4 = mybir.dt.float4_e2m1fn_x4
ALU = mybir.AluOpType

P = 128
PACK = 4
BANK = 512
PASSES = K // (P * PACK)
BLOCKS = N // P
HALVES = T // BANK
WE_PARTS = 2
WE_COLS = N // WE_PARTS


def tile_moe_expert_held_near_shared_kernel(
    tc, xt_words, xt_scales, ws_words, ws_scales, xe_words, xe_scales, we, bd, rw, offs, out
):
    nc = tc.nc
    with ExitStack() as ctx:
        keep = ctx.enter_context(tc.tile_pool(name="keep", bufs=1))
        psum = ctx.enter_context(tc.psum_pool(name="psum", bufs=1))

        offsets = keep.tile([P, J // 16], U16, name="offsets")
        xt_plane = keep.tile([P, PASSES, T], U8, name="xt_plane", align_bytes=64)
        ws_plane = keep.tile([P, PASSES, N], U8, name="ws_plane", align_bytes=64)
        xe_plane = keep.tile([P, 1, J], U8, name="xe_plane", align_bytes=64)
        ws_codes = keep.tile([P, PASSES, 2 * N], U8, name="ws_codes", align_bytes=64)
        xt_codes = [keep.tile([P, PASSES, BANK], U32, name="xt_codes%d" % h, align_bytes=64) for h in range(HALVES)]
        xe_codes = keep.tile([P, J], U32, name="xe_codes", align_bytes=64)
        we_raw = [keep.tile([P, PACK, WE_COLS], F32, name="we_raw%d" % a) for a in range(WE_PARTS)]
        we_bf16 = [keep.tile([P, P, PACK], BF16, name="we_bf16%d" % b, align_bytes=64) for b in range(BLOCKS)]
        we_codes = [keep.tile([P, P], U32, name="we_codes%d" % b, align_bytes=64) for b in range(BLOCKS)]
        we_plane = [keep.tile([P, P], U8, name="we_plane%d" % b, align_bytes=64) for b in range(BLOCKS)]
        vec_rows = keep.tile([P, P], F32, name="vec_rows")
        vec_cols = keep.tile([P, 2 * BLOCKS], F32, name="vec_cols")
        ident = keep.tile([P, P], F32, name="ident")
        u_sb = [keep.tile([P, T], F32, name="u%d" % b) for b in range(BLOCKS)]
        listed = [keep.tile([P, J], F32, name="listed%d" % b) for b in range(BLOCKS)]
        capped = [keep.tile([P, J], F32, name="capped%d" % b) for b in range(BLOCKS)]
        held = [keep.tile([P, J], F32, name="held%d" % b) for b in range(BLOCKS)]
        result = [keep.tile([P, J], F32, name="result%d" % b) for b in range(BLOCKS)]

        def load_scale_rows(engine, plane, scales, r):
            src = scales.rearrange("z (q r) c -> r q z c", r=PACK)[r]
            engine.dma_start(out=plane[r:P:32, :, :].bitcast(I32), in_=src.bitcast(I32))

        nc.vector.memset(ws_plane[:].bitcast(I32), 0)
        nc.vector.memset(xt_plane[:].bitcast(I32), 0)
        nc.sync.dma_start(out=ws_codes[:].bitcast(I32), in_=ws_words.rearrange("z p c -> p z c").bitcast(I32))
        load_scale_rows(nc.sync, ws_plane, ws_scales, 0)
        for r in range(1, PACK):
            load_scale_rows(nc.scalar, ws_plane, ws_scales, r)
        for r in range(PACK - 1):
            load_scale_rows(nc.scalar, xt_plane, xt_scales, r)
        xt_rows = xt_words.rearrange("z p c r -> p z (c r)")
        for h in range(HALVES):
            cols = slice(h * BANK * PACK, (h + 1) * BANK * PACK)
            nc.sync.dma_start(out=xt_codes[h][:].bitcast(I32), in_=xt_rows[:, :, cols].bitcast(I32))
        load_scale_rows(nc.sync, xt_plane, xt_scales, PACK - 1)

        we_rows = we.rearrange("(p j) n -> p j n", j=PACK)
        nc.vector.memset(xe_plane[:].bitcast(I32), 0)
        nc.vector.memset(vec_rows[:], 0.0)
        nc.sync.dma_start(out=we_raw[0][:], in_=we_rows[:, :, 0:WE_COLS])
        nc.sync.dma_start(offsets[:], offs)
        nc.sync.dma_start(out=xe_codes[:].bitcast(I32), in_=xe_words[0].rearrange("p c r -> p (c r)").bitcast(I32))
        for r in range(PACK):
            load_scale_rows(nc.sync, xe_plane, xe_scales, r)
        nc.sync.dma_start(out=vec_rows[0:BLOCKS, :], in_=bd.rearrange("(c p) o -> c (p o)", p=P))
        nc.sync.dma_start(out=vec_rows[BLOCKS : 2 * BLOCKS, :], in_=rw.rearrange("o (c p) -> (o c) p", p=P))
        nc.sync.dma_start(out=we_raw[1][:], in_=we_rows[:, :, WE_COLS:N])
        make_identity(nc, ident[:])

        def bank(name):
            return psum.tile([P, BANK], F32, name=name, tag=name, bufs=1)

        def shared_product(b, h, acc):
            for z in range(PASSES):
                nc.tensor.matmul_mx(
                    out=acc[:],
                    lhsT=ws_codes[:, z, 2 * P * b : 2 * P * (b + 1)].bitcast(FP4X4),
                    lhsT_scale=ws_plane[:, z, P * b : P * (b + 1)],
                    rhs=xt_codes[h][:, z, :].bitcast(FP8X4),
                    rhs_scale=xt_plane[:, z, BANK * h : BANK * (h + 1)],
                    start=(z == 0),
                    stop=(z == PASSES - 1),
                )
            nc.scalar.copy(out=u_sb[b][:, BANK * h : BANK * (h + 1)], in_=acc[:])

        def gather(b):
            nc.vector.tensor_copy(out=listed[b][:], in_=u_sb[b][:].indirect(offsets[:]))

        def round_we(b):
            a, c = divmod(b * P, WE_COLS)
            nc.scalar.copy(
                out=we_bf16[b][:].rearrange("p (c i) j -> p c j i", i=4),
                in_=we_raw[a][:, :, c : c + P].rearrange("p j (c i) -> p c j i", i=4),
            )

        def quantize_we(b):
            nc.vector.quantize_mx(
                out=we_codes[b][:].bitcast(FP8X4),
                scales=we_plane[b][:],
                in_=we_bf16[b][:].rearrange("p c j -> p (c j)"),
            )

        def expert_product(b, acc):
            nc.tensor.matmul_mx(
                out=acc[:],
                lhsT=we_codes[b][:].bitcast(FP8X4),
                lhsT_scale=we_plane[b][:],
                rhs=xe_codes[:].bitcast(FP8X4),
                rhs_scale=xe_plane[:, 0, :],
                start=True,
                stop=True,
            )
            return acc

        def cap(b, p_acc):
            nc.vector.scalar_tensor_tensor(
                out=capped[b][:], in0=listed[b][:], scalar=vec_cols[:, b : b + 1], in1=p_acc[:], op0=ALU.add, op1=ALU.min
            )

        def floor(b):
            nc.vector.scalar_tensor_tensor(
                out=held[b][:], in0=listed[b][:], scalar=vec_cols[:, b : b + 1], in1=capped[b][:], op0=ALU.subtract, op1=ALU.max
            )

        def weigh(b, cols, engine, weights, queue):
            engine.tensor_tensor(out=result[b][:, cols], in0=held[b][:, cols], in1=weights[:, cols], op=ALU.mult)
            queue.dma_start(out=out[P * b : P * (b + 1), cols], in_=result[b][:, cols])

        everything = slice(0, J)
        shared_product(0, 0, bank("bank0"))
        round_we(0)
        quantize_we(0)
        shared_product(0, 1, bank("bank1"))
        gather(0)
        shared_product(1, 0, bank("bank2"))
        shared_product(1, 1, bank("bank3"))
        gather(1)
        p0 = expert_product(0, bank("bank3"))

        vec_t = bank("bank6")
        nc.tensor.transpose(vec_t[:, 0:P], vec_rows[:], ident[:])
        nc.scalar.copy(out=vec_cols[:], in_=vec_t[:, 0 : 2 * BLOCKS])
        round_we(1)
        shared_product(2, 0, bank("bank4"))
        shared_product(2, 1, bank("bank5"))
        rw_all = bank("bank7")
        for c in range(J // P):
            col = vec_cols[:, BLOCKS + c : BLOCKS + c + 1]
            nc.tensor.transpose(rw_all[:, P * c : P * (c + 1)], col.to_broadcast([P, P]), ident[:])
        cap(0, p0)
        quantize_we(1)
        floor(0)
        gather(2)
        p1 = expert_product(1, bank("bank5"))
        round_we(2)
        round_we(3)
        shared_product(3, 0, bank("bank0"))
        shared_product(3, 1, bank("bank1"))
        cap(1, p1)
        quantize_we(2)
        weigh(0, everything, nc.vector, rw_all, nc.sync)
        floor(1)
        quantize_we(3)
        gather(3)
        weigh(1, everything, nc.vector, rw_all, nc.sync)
        p2 = expert_product(2, bank("bank1"))
        p3 = expert_product(3, bank("bank0"))
        cap(2, p2)
        cap(3, p3)
        floor(2)
        floor(3)
        weigh(2, everything, nc.vector, rw_all, nc.sync)
        weigh(3, slice(0, J // 2), nc.vector, rw_all, nc.scalar)
        weigh(3, slice(J // 2, J), nc.vector, rw_all, nc.sync)
